import numpy as np, ml_dtypes
CORES = [0,1,2,3]
N = 4
def setup_inputs(rng):
    return {"x": rng.standard_normal((N, 128, 8), dtype=np.float32).astype(ml_dtypes.bfloat16)}
def reference(x):
    g = np.ascontiguousarray(x.transpose(1, 2, 0)).reshape(128, 8 * N)
    return {"y": np.broadcast_to(g, (N,) + g.shape)}

from concourse.bass import DstId, RemoteDMATransfer

N = 4
COLS = 8
OWN = COLS // N
BLK = OWN * N

SCRATCH = {
    "mine": ("sbuf", [128, COLS], "bfloat16"),
    "stage": ("sbuf", [128, COLS * N], "bfloat16"),
}
SEMAPHORES = ["loaded", "own", "scat", "gath", "stored"]


def scatter_plan(rank):
    cols = [j for j in range(COLS) if j // OWN != rank]
    first = [(j, 0xF << (4 * i), 4) for i, j in enumerate(cols[:4])]
    second = [(j, 0xFF << (8 * i), 8) for i, j in enumerate(cols[4:])]
    return [first, second]


def rank_program(g, core, T, topo):
    rank = T.rank_of(core)
    if rank is None:
        return

    def dst_id(r):
        rid, pid, _se = topo.addr(T.cores[r])
        return DstId(rid=rid, pnc=pid)

    peers = [r for r in range(N) if r != rank]
    lo = rank * BLK

    g.sync.dma_start(T.mine[:], T.x[:]).then_inc(T.sem.loaded, 16)
    g.dma_start(T.stage[:, lo + rank:lo + BLK:N], T.x[:, rank * OWN:(rank + 1) * OWN],
                allow_slow_non_contiguous=True).then_inc(T.sem.own, 16)

    g.wait_ge(T.sem.loaded, 16)
    left = 0
    for call in scatter_plan(rank):
        g.remote_dma_fused([
            RemoteDMATransfer(
                dst_ids=[dst_id(j // OWN)], dma_engine_mask=m, remote_sem=T.sem.scat,
                srcs=[T.mine[:, j:j + 1]], dsts=[T.stage[:, j * N + rank:j * N + rank + 1]])
            for j, m, _n in call], local_sem=T.sem.gath)
        left += sum(n for _j, _m, n in call)

    due = sum(n for r in peers for call in scatter_plan(r) for j, _m, n in call if j // OWN == rank)
    g.wait_ge(T.sem.scat, due)
    g.wait_ge(T.sem.own, 16)
    g.remote_dma_fused([
        RemoteDMATransfer(
            dst_ids=[dst_id(r) for r in peers], dma_engine_mask=0xFFFF, remote_sem=T.sem.gath,
            srcs=[T.stage[:, lo:lo + BLK]], dsts=[T.stage[:, lo:lo + BLK] for _r in peers])],
        local_sem=T.sem.gath)
    left += 16

    g.sync.wait_ge(T.sem.scat, due)
    g.sync.wait_ge(T.sem.own, 16)
    g.sync.wait_ge(T.sem.gath, 16 * len(peers) + left)
    g.sync.dma_start(T.y[:], T.stage[:]).then_inc(T.sem.stored, 16)
    g.wait_ge(T.sem.stored, 16)
